import numpy as np, ml_dtypes
CORES = [2,34,66,98,130,162,194,226,258,290,322,354,386,418,450,482]
N = 16
T = 1024
def entries(a): return a.T.reshape(-1)
def pack(v, P): return np.ascontiguousarray(np.asarray(v, np.int32).reshape(-1, P).T)
def lists(rng, how):
    h = rng.integers(0, N * T, 8)
    if how == "zero": h[:] = 0
    if how == "blocks": h = T * rng.integers(1, N, 8)
    if how == "last": h[:] = N * T - 1
    if how == "mixed": h = T * rng.choice([q for q in range(N) if q & (q - 1)], 8) + rng.integers(1, T, 8)
    if how == "small": h = rng.permutation([0, 1, T - 1, T, T + 1, N * T - 1, T * int(rng.integers(2, N)), int(rng.integers(1, T))])
    return {"hh": np.broadcast_to(pack(np.concatenate([h, np.zeros(24, np.int64)]), 16), (N, 16, 2)).copy()}
def setup_inputs(rng):
    return dict({"x": rng.standard_normal((N, 128, T), dtype=np.float32).astype(ml_dtypes.bfloat16)}, **lists(rng, "uniform"))
def setup_inputs_blocks(rng):
    d = setup_inputs(rng); d.update(lists(rng, "blocks"))
    for k in ("x",): d[k] = (d[k].astype(np.float32) * 1048576.0).astype(d[k].dtype)
    return d
def setup_inputs_last(rng):
    d = setup_inputs(rng); d.update(lists(rng, "last"))
    for k in ("x",): d[k] = (d[k].astype(np.float32) * (1 / 1024.0)).astype(d[k].dtype)
    return d
def setup_inputs_mixed(rng):
    d = setup_inputs(rng); d.update(lists(rng, "mixed"))
    return d
def setup_inputs_small(rng):
    d = setup_inputs(rng); d.update(lists(rng, "small"))
    return d
def setup_inputs_zero(rng):
    d = setup_inputs(rng); d.update(lists(rng, "zero"))
    return d
def check_inputs(x):
    bad = []
    if x["hh"].min() < 0 or x["hh"].max() >= N * T: bad.append("hh out of range")
    if entries(x["hh"][0])[8:].any(): bad.append("an entry that should be 0 isn't")
    if not all(np.array_equal(a, x["hh"][0]) for a in x["hh"]): bad.append("hh isn't alike on all ranks")
    return bad
def reference(x, hh):
    h = entries(hh[0]); A = np.concatenate(list(x), axis=1)
    Y = np.concatenate([np.roll(A[16 * k:16 * k + 16], -int(h[k]), axis=1) for k in range(8)], axis=0)
    return {"y": np.stack([Y[:, T * r:T * r + T] for r in range(N)])}

@@ -1,0 +1,191 @@
+from concourse.bass import DstId, RemoteDMATransfer
+from concourse.mybir import AluOpType, ActivationFunctionType
+
+N, W, C = 16, 1024, 128
+NS = W // C
+
+SCRATCH = {
+    "xs": ("dram", [NS, 128, C], "bfloat16"),
+    "stage": ("dram", [128, C], "bfloat16"),
+    "ring": ("sbuf", [128, N * C], "bfloat16"),
+    "po": ("sbuf", [128, W], "bfloat16"),
+    "v": ("sbuf", [128, W], "bfloat16"),
+    "yb": ("sbuf", [128, W], "bfloat16"),
+    "hhs": ("sbuf", [128, 8], "int32"),
+    "hf": ("sbuf", [128, 8], "float32"),
+    "pcol": ("sbuf", [128, 8], "int32"),
+    "rc": ("sbuf", [128, 8], "int32"),
+    "rf": ("sbuf", [128, 8], "float32"),
+    "s1": ("sbuf", [128, 8], "float32"),
+    "s2": ("sbuf", [128, 8], "float32"),
+    "si": ("sbuf", [128, 128], "int32"),
+    "sh": ("sbuf", [128, 128], "int32"),
+    "sel": ("sbuf", [128, 128], "float32"),
+    "ib1": ("sbuf", [128, 64], "int32"),
+    "ib2": ("sbuf", [128, 64], "int32"),
+    "ic": ("sbuf", [128, 64], "int32"),
+    "cc": ("sbuf", [128, 64], "int32"),
+    "a1": ("sbuf", [128, 64], "int32"),
+    "b1": ("sbuf", [128, 64], "int32"),
+    "d1": ("sbuf", [128, 64], "int32"),
+    "a2": ("sbuf", [128, 64], "int32"),
+    "b2": ("sbuf", [128, 64], "int32"),
+    "off1": ("sbuf", [128, 64], "uint16"),
+    "off2": ("sbuf", [128, 64], "uint16"),
+    "hp": ("psum", [128, 8], "float32"),
+}
+SEMAPHORES = ["ld", "hl", "gi", "vl", "mm", "arr", "ringed", "pv", "ps", "vin", "rv", "rs", "st", "snt"]
+
+
+def bits(mask):
+    return [1 << b for b in range(16) if mask >> b & 1]
+
+
+def spread(mask, n):
+    b = bits(mask)
+    return sum(b[::len(b) // n][:n])
+
+
+def plan(T, topo):
+    cores = [int(c) for c in T.cores]
+    rk = [topo.rack(topo.host(c)) for c in cores]
+    peers = [[s for s in range(N) if rk[s] == rk[r]] for r in range(N)]
+    partner = [[s for s in range(N) if rk[s] != rk[r] and topo.chip(cores[s]) == topo.chip(cores[r])
+                and topo.may_write(cores[r], cores[s])][0] for r in range(N)]
+    slc = [peers[r].index(r) if rk[r] == rk[0] else peers[0].index(partner[r]) for r in range(N)]
+    where = {}
+    for r in range(N):
+        where[(topo.host(cores[r]), topo.chip(cores[r]))] = r
+    span = max(cores) + 128
+    helpers = [[] for _ in range(N)]
+    for c in range(min(span, 512)):
+        r = where.get((topo.host(c), topo.chip(c)))
+        if r is not None and c != cores[r]:
+            helpers[r].append(c)
+    helper = [dict(zip([s for s in peers[r] if s != r], helpers[r])) for r in range(N)]
+    return cores, peers, partner, slc, helper
+
+
+def send(T, topo, src_core, dst_core, mask, sem, src, dst):
+    rid, pid = topo.addr(dst_core, src_core)
+    return RemoteDMATransfer(dst_ids=[DstId(rid=rid, pnc=pid)], dma_engine_mask=mask, remote_sem=sem, src=src, dst=dst)
+
+
+NA, NB = 4, 4
+
+
+def helper_program(g, core, r, s, T, topo, cores, partner):
+    far, near = cores[partner[r]], cores[r]
+    m_far = topo.mask(core, far)
+    m_near = topo.mask(core, near) & ~m_far
+    slot = T.ring[:, s * C:(s + 1) * C]
+    g.wait_ge(T.sem.arr, 1)
+    g.remote_dma_fused([
+        send(T, topo, core, far, spread(m_far, NA), T.sem.ringed, T.stage[:], slot),
+        send(T, topo, core, near, spread(m_near, NB), T.sem.ringed, T.stage[:], slot),
+    ], local_sem=T.sem.snt)
+    g.wait_ge(T.sem.snt, NA + NB)
+
+
+def rank_program(g, core, T, topo):
+    cores, peers, partner, slc, helper = plan(T, topo)
+    r = T.rank_of(core)
+    if r is None:
+        for q in range(N):
+            for s in helper[q]:
+                if helper[q][s] == core:
+                    helper_program(g, core, q, s, T, topo, cores, partner)
+        return
+    S = T.sem
+    V = g.vector
+    m, mine = slc[r], peers[r]
+    others = [d for d in mine if d != r]
+    own_slot = T.ring[:, r * C:(r + 1) * C]
+
+    k = 0
+    for d in others + [r]:
+        q = (g.sync, g.scalar)[k % 2]
+        k += 1
+        n = slc[d]
+        q.dma_start(own_slot if d == r else T.xs[n], T.x[:, n * C:(n + 1) * C]).then_inc(S.ld, 16)
+    g.sync.dma_start(T.hhs[0:16, 0:2], T.hh[:]).then_inc(S.hl, 16)
+
+    d0 = mine[0]
+    g.iota(T.pcol[:, 0:1], [[1, 1]], 0, 1).then_inc(S.gi, 1)
+    g.iota(T.si[0:16, :], [[1, 128]], 0, -16).then_inc(S.gi, 1)
+    g.iota(T.ic[:], [[0, 8], [16, 8]], 0, 0).then_inc(S.gi, 1)
+    g.iota(T.ib1[:], [[W, 8], [-16, 8]], W * d0 + W - 1 - C * m, 0).then_inc(S.gi, 1)
+    g.iota(T.ib2[:], [[16, 64]], 0, 0).then_inc(S.gi, 1)
+
+    g.wait_ge(S.ld, 16 * NS)
+    far = cores[partner[r]]
+    tr, left = [], bits(topo.mask(core, far))
+    for d in others:
+        h = helper[d][r]
+        tr.append(send(T, topo, core, h, left.pop(0), S.arr, T.xs[slc[d]], T.stage[:]))
+    tr.append(send(T, topo, core, far, left.pop(0), S.ringed, own_slot, own_slot))
+    g.remote_dma_fused(tr, local_sem=S.snt)
+
+    n = [0]
+
+    def step(ins):
+        ins.then_inc(S.vl, 1)
+        n[0] += 1
+        V.wait_ge(S.vl, n[0])
+
+    A = AluOpType
+    V.wait_ge(S.gi, 5)
+    step(V.tensor_scalar(T.rc[:, 0:1], T.pcol[:, 0:1], 15, None, A.bitwise_and))
+    step(V.tensor_copy(T.rf[:, 0:1], T.rc[:, 0:1]))
+    step(V.tensor_scalar(T.sh[0:16, :], T.si[0:16, :], 4, None, A.arith_shift_right))
+    step(V.tensor_scalar(T.sel[0:16, :], T.sh[0:16, :], 0, None, A.is_equal))
+    step(V.tensor_scalar(T.cc[:], T.ic[:], T.rf[:, 0:1], None, A.add))
+    V.wait_ge(S.hl, 16)
+    step(V.tensor_copy(T.hf[0:16, 0:2], T.hhs[0:16, 0:2]))
+    g.tensor.wait_ge(S.vl, n[0])
+    g.tensor.matmul(T.hp[:, 0:1], T.sel[0:16, :], T.hf[0:16, 0:1], True, True).then_inc(S.mm, 1)
+    V.wait_ge(S.mm, 1)
+    step(V.tensor_tensor(T.s1[:, 0:1], T.hp[:, 0:1], T.rf[:, 0:1], A.subtract))
+    step(V.tensor_tensor(T.s2[:, 0:1], T.hp[:, 0:1], T.rf[:, 0:1], A.add))
+    step(V.tensor_scalar(T.a1[:], T.ib1[:], T.s1[:, 0:1], None, A.add))
+    step(V.tensor_scalar(T.b1[:], T.a1[:], 3, (N - 1) * C, A.arith_shift_right, A.bitwise_and))
+    step(V.tensor_tensor(T.d1[:], T.b1[:], T.cc[:], A.add))
+    step(V.tensor_copy(T.off1[:], T.d1[:]))
+    step(V.tensor_scalar(T.a2[:], T.ib2[:], T.s2[:, 0:1], None, A.add))
+    step(V.tensor_scalar(T.b2[:], T.a2[:], W - 1, None, A.bitwise_and))
+    step(V.tensor_copy(T.off2[:], T.b2[:]))
+    listed = n[0]
+
+    arrivals = len(others) * (NA + NB) + 1
+    half = W // 2
+    copy = ActivationFunctionType.Copy
+    for q in (V, g.scalar):
+        q.wait_ge(S.ld, 16 * NS)
+        q.wait_ge(S.ringed, arrivals)
+    g.scalar.wait_ge(S.vl, listed)
+    V.tensor_copy(T.po[:, 0:half], T.ring[:, 0:N * C].indirect(T.off1[:, 0:32])).then_inc(S.pv, 1)
+    g.scalar.activation(T.po[:, half:W], T.ring[:, 0:N * C].indirect(T.off1[:, 32:64]), copy, bias=-0.0).then_inc(S.ps, 1)
+
+    g.wait_ge(S.pv, 1)
+    g.wait_ge(S.ps, 1)
+    tr, left = [], bits(topo.mask(core, cores[others[0]]))
+    for d in others:
+        e = mine.index(d)
+        tr.append(send(T, topo, core, cores[d], left.pop(0), S.vin, T.po[:, e * C:(e + 1) * C], T.v[:, m * C:(m + 1) * C]))
+    g.remote_dma_fused(tr, local_sem=S.snt)
+    V.wait_ge(S.pv, 1)
+    V.wait_ge(S.ps, 1)
+    e = mine.index(r)
+    step(V.tensor_copy(T.v[:, m * C:(m + 1) * C], T.po[:, e * C:(e + 1) * C]))
+
+    g.scalar.wait_ge(S.vl, n[0])
+    for q in (V, g.scalar):
+        q.wait_ge(S.vin, len(others))
+    V.tensor_copy(T.yb[:, 0:half], T.v[:, 0:W].indirect(T.off2[:, 0:32])).then_inc(S.rv, 1)
+    g.scalar.activation(T.yb[:, half:W], T.v[:, 0:W].indirect(T.off2[:, 32:64]), copy, bias=-0.0).then_inc(S.rs, 1)
+    g.sync.wait_ge(S.rv, 1)
+    g.sync.dma_start(T.y[:, 0:half], T.yb[:, 0:half]).then_inc(S.st, 16)
+    g.scalar.wait_ge(S.rs, 1)
+    g.scalar.dma_start(T.y[:, half:W], T.yb[:, half:W]).then_inc(S.st, 16)
+    g.sync.wait_ge(S.st, 32)
+    g.wait_ge(S.snt, 2 * len(others) + 1)

@@ -6,7 +6,7 @@ NS = W // C
 
 SCRATCH = {
     "xs": ("dram", [NS, 128, C], "bfloat16"),
-    "stage": ("dram", [128, C], "bfloat16"),
+    "stage": ("dram", [2, 128, C], "bfloat16"),
     "ring": ("sbuf", [128, N * C], "bfloat16"),
     "po": ("sbuf", [128, W], "bfloat16"),
     "v": ("sbuf", [128, W], "bfloat16"),
@@ -16,8 +16,6 @@ SCRATCH = {
     "pcol": ("sbuf", [128, 8], "int32"),
     "rc": ("sbuf", [128, 8], "int32"),
     "rf": ("sbuf", [128, 8], "float32"),
-    "s1": ("sbuf", [128, 8], "float32"),
-    "s2": ("sbuf", [128, 8], "float32"),
     "si": ("sbuf", [128, 128], "int32"),
     "sh": ("sbuf", [128, 128], "int32"),
     "sel": ("sbuf", [128, 128], "float32"),
@@ -34,7 +32,13 @@ SCRATCH = {
     "off2": ("sbuf", [128, 64], "uint16"),
     "hp": ("psum", [128, 8], "float32"),
 }
-SEMAPHORES = ["ld", "hl", "gi", "vl", "mm", "arr", "ringed", "pv", "ps", "vin", "rv", "rs", "st", "snt"]
+SEMAPHORES = ["ld0", "ld1", "ld2", "hl", "gi", "vl", "mm", "arr0", "arr1", "ringed", "c0", "c1", "own", "vin",
+              "r0", "r1", "r2", "r3", "st", "snt"]
+
+NA, NB = 4, 4
+CALLS1 = [(False, 4, 2), (True, 3, 2)]
+CALLS3 = [(4, 2), (3, 2)]
+PARTS = 4
 
 
 def bits(mask):
@@ -46,6 +50,13 @@ def spread(mask, n):
     return sum(b[::len(b) // n][:n])
 
 
+def engines1(k):
+    for own, n, e in CALLS1:
+        if k < n:
+            return e
+        k -= n
+
+
 def plan(T, topo):
     cores = [int(c) for c in T.cores]
     rk = [topo.rack(topo.host(c)) for c in cores]
@@ -53,139 +64,178 @@ def plan(T, topo):
     partner = [[s for s in range(N) if rk[s] != rk[r] and topo.chip(cores[s]) == topo.chip(cores[r])
                 and topo.may_write(cores[r], cores[s])][0] for r in range(N)]
     slc = [peers[r].index(r) if rk[r] == rk[0] else peers[0].index(partner[r]) for r in range(N)]
-    where = {}
-    for r in range(N):
-        where[(topo.host(cores[r]), topo.chip(cores[r]))] = r
-    span = max(cores) + 128
-    helpers = [[] for _ in range(N)]
-    for c in range(min(span, 512)):
+    where = {(topo.host(cores[r]), topo.chip(cores[r])): r for r in range(N)}
+    mates = [[] for _ in range(N)]
+    for c in range(512):
         r = where.get((topo.host(c), topo.chip(c)))
         if r is not None and c != cores[r]:
-            helpers[r].append(c)
-    helper = [dict(zip([s for s in peers[r] if s != r], helpers[r])) for r in range(N)]
-    return cores, peers, partner, slc, helper
+            mates[r].append(c)
+    order = []
+    for s in range(N):
+        p = peers[s]
+        i = p.index(s)
+        order.append([p[(i + o) % NS] for o in range(1, NS)])
+    helper = []
+    for d in range(N):
+        far = {}
+        late = [s for s in peers[d] if s != d and order[s].index(d) >= NS - 1 - CALLS1[-1][1]]
+        first = [s for s in peers[d] if s != d and s not in late]
+        hs = sorted(mates[d][::2], key=lambda c: -abs(c - cores[d]))
+        for w, src in ((0, first), (1, late)):
+            for s, c in zip(src, hs):
+                far[s] = (c, w)
+        helper.append(far)
+    return cores, peers, partner, slc, order, helper
 
 
-def send(T, topo, src_core, dst_core, mask, sem, src, dst):
+def send(topo, src_core, dst_core, mask, sem, src, dst):
     rid, pid = topo.addr(dst_core, src_core)
     return RemoteDMATransfer(dst_ids=[DstId(rid=rid, pnc=pid)], dma_engine_mask=mask, remote_sem=sem, src=src, dst=dst)
 
 
-NA, NB = 4, 4
-
-
-def helper_program(g, core, r, s, T, topo, cores, partner):
+def helper_program(g, core, r, jobs, T, topo, cores, partner, order):
     far, near = cores[partner[r]], cores[r]
     m_far = topo.mask(core, far)
     m_near = topo.mask(core, near) & ~m_far
-    slot = T.ring[:, s * C:(s + 1) * C]
-    g.wait_ge(T.sem.arr, 1)
-    g.remote_dma_fused([
-        send(T, topo, core, far, spread(m_far, NA), T.sem.ringed, T.stage[:], slot),
-        send(T, topo, core, near, spread(m_near, NB), T.sem.ringed, T.stage[:], slot),
-    ], local_sem=T.sem.snt)
-    g.wait_ge(T.sem.snt, NA + NB)
+    for w, s in jobs:
+        slot = T.ring[:, s * C:(s + 1) * C]
+        g.wait_ge(T.sem["arr%d" % w], engines1(order[s].index(r)))
+        g.remote_dma_fused([
+            send(topo, core, far, spread(m_far, NA), T.sem.ringed, T.stage[w], slot),
+            send(topo, core, near, spread(m_near, NB), T.sem.ringed, T.stage[w], slot),
+        ], local_sem=T.sem.snt)
+    g.wait_ge(T.sem.snt, (NA + NB) * len(jobs))
 
 
 def rank_program(g, core, T, topo):
-    cores, peers, partner, slc, helper = plan(T, topo)
+    cores, peers, partner, slc, order, helper = plan(T, topo)
     r = T.rank_of(core)
     if r is None:
         for q in range(N):
-            for s in helper[q]:
-                if helper[q][s] == core:
-                    helper_program(g, core, q, s, T, topo, cores, partner)
+            jobs = sorted((helper[q][s][1], s) for s in helper[q] if helper[q][s][0] == core)
+            if jobs:
+                helper_program(g, core, q, jobs, T, topo, cores, partner, order)
         return
     S = T.sem
-    V = g.vector
-    m, mine = slc[r], peers[r]
-    others = [d for d in mine if d != r]
+    V, A = g.vector, g.scalar
+    m, mine, dests = slc[r], peers[r], order[r]
     own_slot = T.ring[:, r * C:(r + 1) * C]
+    calls = []
+    k = 0
+    for own, cnt, eng in CALLS1:
+        calls.append((dests[k:k + cnt] + ([r] if own else []), eng))
+        k += cnt
 
     k = 0
-    for d in others + [r]:
-        q = (g.sync, g.scalar)[k % 2]
-        k += 1
-        n = slc[d]
-        q.dma_start(own_slot if d == r else T.xs[n], T.x[:, n * C:(n + 1) * C]).then_inc(S.ld, 16)
+    for j, (ds, eng) in enumerate(calls):
+        for d in ds:
+            out = own_slot if d == r else T.xs[slc[d]]
+            (g.sync, A)[k % 2].dma_start(out, T.x[:, C * slc[d]:C * slc[d] + C]).then_inc(S["ld%d" % j], 16)
+            k += 1
     g.sync.dma_start(T.hhs[0:16, 0:2], T.hh[:]).then_inc(S.hl, 16)
 
     d0 = mine[0]
     g.iota(T.pcol[:, 0:1], [[1, 1]], 0, 1).then_inc(S.gi, 1)
     g.iota(T.si[0:16, :], [[1, 128]], 0, -16).then_inc(S.gi, 1)
     g.iota(T.ic[:], [[0, 8], [16, 8]], 0, 0).then_inc(S.gi, 1)
-    g.iota(T.ib1[:], [[W, 8], [-16, 8]], W * d0 + W - 1 - C * m, 0).then_inc(S.gi, 1)
+    up = NS - 1 - mine.index(r)
+    if up:
+        g.iota(T.ib1[:, 0:8 * up], [[W, up], [-16, 8]], W * (r + 1) + W - 1 - C * m, 0).then_inc(S.gi, 1)
+    g.iota(T.ib1[:, 8 * up:64], [[W, NS - up], [-16, 8]], W * d0 + W - 1 - C * m, 0).then_inc(S.gi, 1)
     g.iota(T.ib2[:], [[16, 64]], 0, 0).then_inc(S.gi, 1)
+    made = 6 if up else 5
 
-    g.wait_ge(S.ld, 16 * NS)
     far = cores[partner[r]]
-    tr, left = [], bits(topo.mask(core, far))
-    for d in others:
-        h = helper[d][r]
-        tr.append(send(T, topo, core, h, left.pop(0), S.arr, T.xs[slc[d]], T.stage[:]))
-    tr.append(send(T, topo, core, far, left.pop(0), S.ringed, own_slot, own_slot))
-    g.remote_dma_fused(tr, local_sem=S.snt)
+    own_engines = [eng for ds, eng in calls if r in ds][0]
+    sent = 0
+    for j, (ds, eng) in enumerate(calls):
+        g.wait_ge(S["ld%d" % j], 16 * len(ds))
+        tr = []
+        for d in ds:
+            c, hw = (far, None) if d == r else helper[d][r]
+            b = bits(topo.mask(core, c))[eng * len(tr):eng * len(tr) + eng]
+            if d == r:
+                tr.append(send(topo, core, c, sum(b), S.ringed, own_slot, own_slot))
+            else:
+                tr.append(send(topo, core, c, sum(b), S["arr%d" % hw], T.xs[slc[d]], T.stage[hw]))
+        g.remote_dma_fused(tr, local_sem=S.snt)
+        sent += eng * len(tr)
 
     n = [0]
 
-    def step(ins):
-        ins.then_inc(S.vl, 1)
-        n[0] += 1
+    def step(*instructions):
+        for ins in instructions:
+            ins.then_inc(S.vl, 1)
+        n[0] += len(instructions)
         V.wait_ge(S.vl, n[0])
 
-    A = AluOpType
-    V.wait_ge(S.gi, 5)
-    step(V.tensor_scalar(T.rc[:, 0:1], T.pcol[:, 0:1], 15, None, A.bitwise_and))
-    step(V.tensor_copy(T.rf[:, 0:1], T.rc[:, 0:1]))
-    step(V.tensor_scalar(T.sh[0:16, :], T.si[0:16, :], 4, None, A.arith_shift_right))
-    step(V.tensor_scalar(T.sel[0:16, :], T.sh[0:16, :], 0, None, A.is_equal))
-    step(V.tensor_scalar(T.cc[:], T.ic[:], T.rf[:, 0:1], None, A.add))
+    O = AluOpType
+    V.wait_ge(S.gi, made)
+    step(V.tensor_scalar(T.rc[:, 0:1], T.pcol[:, 0:1], 15, None, O.bitwise_and),
+         V.tensor_scalar(T.sh[0:16, :], T.si[0:16, :], 4, None, O.arith_shift_right))
+    step(V.tensor_copy(T.rf[:, 0:1], T.rc[:, 0:1]),
+         V.tensor_scalar(T.sel[0:16, :], T.sh[0:16, :], 0, None, O.is_equal))
+    step(V.tensor_scalar(T.cc[:], T.ic[:], T.rf[:, 0:1], None, O.add))
     V.wait_ge(S.hl, 16)
     step(V.tensor_copy(T.hf[0:16, 0:2], T.hhs[0:16, 0:2]))
     g.tensor.wait_ge(S.vl, n[0])
     g.tensor.matmul(T.hp[:, 0:1], T.sel[0:16, :], T.hf[0:16, 0:1], True, True).then_inc(S.mm, 1)
     V.wait_ge(S.mm, 1)
-    step(V.tensor_tensor(T.s1[:, 0:1], T.hp[:, 0:1], T.rf[:, 0:1], A.subtract))
-    step(V.tensor_tensor(T.s2[:, 0:1], T.hp[:, 0:1], T.rf[:, 0:1], A.add))
-    step(V.tensor_scalar(T.a1[:], T.ib1[:], T.s1[:, 0:1], None, A.add))
-    step(V.tensor_scalar(T.b1[:], T.a1[:], 3, (N - 1) * C, A.arith_shift_right, A.bitwise_and))
-    step(V.tensor_tensor(T.d1[:], T.b1[:], T.cc[:], A.add))
+    step(V.tensor_scalar(T.a1[:], T.ib1[:], T.hp[:, 0:1], T.rf[:, 0:1], O.add, O.subtract),
+         V.tensor_scalar(T.a2[:], T.ib2[:], T.hp[:, 0:1], T.rf[:, 0:1], O.add, O.add))
+    step(V.tensor_scalar(T.b1[:], T.a1[:], 3, (N - 1) * C, O.arith_shift_right, O.bitwise_and),
+         V.tensor_scalar(T.b2[:], T.a2[:], W - 1, None, O.bitwise_and))
+    step(V.tensor_tensor(T.d1[:], T.b1[:], T.cc[:], O.add),
+         V.tensor_copy(T.off2[:], T.b2[:]))
     step(V.tensor_copy(T.off1[:], T.d1[:]))
-    step(V.tensor_scalar(T.a2[:], T.ib2[:], T.s2[:, 0:1], None, A.add))
-    step(V.tensor_scalar(T.b2[:], T.a2[:], W - 1, None, A.bitwise_and))
-    step(V.tensor_copy(T.off2[:], T.b2[:]))
     listed = n[0]
 
-    arrivals = len(others) * (NA + NB) + 1
-    half = W // 2
     copy = ActivationFunctionType.Copy
-    for q in (V, g.scalar):
-        q.wait_ge(S.ld, 16 * NS)
-        q.wait_ge(S.ringed, arrivals)
-    g.scalar.wait_ge(S.vl, listed)
-    V.tensor_copy(T.po[:, 0:half], T.ring[:, 0:N * C].indirect(T.off1[:, 0:32])).then_inc(S.pv, 1)
-    g.scalar.activation(T.po[:, half:W], T.ring[:, 0:N * C].indirect(T.off1[:, 32:64]), copy, bias=-0.0).then_inc(S.ps, 1)
 
-    g.wait_ge(S.pv, 1)
-    g.wait_ge(S.ps, 1)
-    tr, left = [], bits(topo.mask(core, cores[others[0]]))
-    for d in others:
-        e = mine.index(d)
-        tr.append(send(T, topo, core, cores[d], left.pop(0), S.vin, T.po[:, e * C:(e + 1) * C], T.v[:, m * C:(m + 1) * C]))
-    g.remote_dma_fused(tr, local_sem=S.snt)
-    V.wait_ge(S.pv, 1)
-    V.wait_ge(S.ps, 1)
-    e = mine.index(r)
-    step(V.tensor_copy(T.v[:, m * C:(m + 1) * C], T.po[:, e * C:(e + 1) * C]))
+    def by_v(out, win, off, a, b):
+        return V.tensor_copy(out, win.indirect(off[:, a // 16:b // 16]))
 
-    g.scalar.wait_ge(S.vl, n[0])
-    for q in (V, g.scalar):
-        q.wait_ge(S.vin, len(others))
-    V.tensor_copy(T.yb[:, 0:half], T.v[:, 0:W].indirect(T.off2[:, 0:32])).then_inc(S.rv, 1)
-    g.scalar.activation(T.yb[:, half:W], T.v[:, 0:W].indirect(T.off2[:, 32:64]), copy, bias=-0.0).then_inc(S.rs, 1)
-    g.sync.wait_ge(S.rv, 1)
-    g.sync.dma_start(T.y[:, 0:half], T.yb[:, 0:half]).then_inc(S.st, 16)
-    g.scalar.wait_ge(S.rs, 1)
-    g.scalar.dma_start(T.y[:, half:W], T.yb[:, half:W]).then_inc(S.st, 16)
-    g.sync.wait_ge(S.st, 32)
-    g.wait_ge(S.snt, 2 * len(others) + 1)
+    def by_a(out, win, off, a, b):
+        return A.activation(out, win.indirect(off[:, a // 16:b // 16]), copy, bias=-0.0)
+
+    own_load = [j for j, (ds, eng) in enumerate(calls) if r in ds][0]
+    for q in (V, A):
+        q.wait_ge(S["ld%d" % own_load], 16 * len(calls[own_load][0]))
+        q.wait_ge(S.ringed, len(dests) * (NA + NB) + own_engines)
+    A.wait_ge(S.vl, listed)
+    ring = T.ring[:, 0:N * C]
+    lo = 0
+    for j, (cnt, eng) in enumerate(CALLS3):
+        hi = lo + C * cnt
+        mid = lo + (hi - lo) // 64 * 32
+        by_v(T.po[:, lo:mid], ring, T.off1, lo, mid).then_inc(S["c%d" % j], 1)
+        by_a(T.po[:, mid:hi], ring, T.off1, mid, hi).then_inc(S["c%d" % j], 1)
+        lo = hi
+    by_v(T.v[:, m * C:(m + 1) * C], ring, T.off1, lo, W).then_inc(S.own, 1)
+
+    e = 0
+    for j, (cnt, eng) in enumerate(CALLS3):
+        g.wait_ge(S["c%d" % j], 2)
+        tr = []
+        for d in dests[e:e + cnt]:
+            b = bits(topo.mask(core, cores[d]))[eng * len(tr):eng * len(tr) + eng]
+            tr.append(send(topo, core, cores[d], sum(b), S.vin, T.po[:, e * C:(e + 1) * C], T.v[:, m * C:(m + 1) * C]))
+            e += 1
+        g.remote_dma_fused(tr, local_sem=S.snt)
+        sent += eng * cnt
+
+    got = sum(cnt * eng for cnt, eng in CALLS3)
+    for q in (V, A):
+        q.wait_ge(S.own, 1)
+        q.wait_ge(S.vin, got)
+    Q = W // PARTS
+    v = T.v[:, 0:W]
+    for k in range(PARTS):
+        a, b = k * Q, (k + 1) * Q
+        (by_v, by_a)[k % 2](T.yb[:, a:b], v, T.off2, a, b).then_inc(S["r%d" % k], 1)
+    for k in range(PARTS):
+        q = A if k == PARTS - 1 else g.sync
+        q.wait_ge(S["r%d" % k], 1)
+        q.dma_start(T.y[:, k * Q:(k + 1) * Q], T.yb[:, k * Q:(k + 1) * Q]).then_inc(S.st, 16)
+    g.sync.wait_ge(S.st, 16 * PARTS)
+    g.wait_ge(S.snt, sent)

@@ -3,6 +3,7 @@ from concourse.mybir import AluOpType, ActivationFunctionType
 
 N, W, C = 16, 1024, 128
 NS = W // C
+O = AluOpType
 
 SCRATCH = {
     "xs": ("dram", [NS, 128, C], "bfloat16"),
@@ -16,13 +17,13 @@ SCRATCH = {
     "pcol": ("sbuf", [128, 8], "int32"),
     "rc": ("sbuf", [128, 8], "int32"),
     "rf": ("sbuf", [128, 8], "float32"),
+    "raw": ("sbuf", [128, 64], "int32"),
     "si": ("sbuf", [128, 128], "int32"),
     "sh": ("sbuf", [128, 128], "int32"),
     "sel": ("sbuf", [128, 128], "float32"),
-    "ib1": ("sbuf", [128, 64], "int32"),
-    "ib2": ("sbuf", [128, 64], "int32"),
-    "ic": ("sbuf", [128, 64], "int32"),
-    "cc": ("sbuf", [128, 64], "int32"),
+    "t1": ("sbuf", [128, 64], "int32"),
+    "tc": ("sbuf", [128, 64], "int32"),
+    "t2": ("sbuf", [128, 64], "int32"),
     "a1": ("sbuf", [128, 64], "int32"),
     "b1": ("sbuf", [128, 64], "int32"),
     "d1": ("sbuf", [128, 64], "int32"),
@@ -32,10 +33,11 @@ SCRATCH = {
     "off2": ("sbuf", [128, 64], "uint16"),
     "hp": ("psum", [128, 8], "float32"),
 }
-SEMAPHORES = ["ld0", "ld1", "ld2", "hl", "gi", "vl", "mm", "arr0", "arr1", "ringed", "c0", "c1", "own", "vin",
+SEMAPHORES = ["ld0", "ld1", "ld2", "hl", "gi", "vl", "mm", "arr0", "arr1", "ringed", "cst", "c0", "c1", "own", "vin",
               "r0", "r1", "r2", "r3", "st", "snt"]
 
 NA, NB = 4, 4
+TABLES = ["t1", "sel", "tc", "t2"]
 CALLS1 = [(False, 4, 2), (True, 3, 2)]
 CALLS3 = [(4, 2), (3, 2)]
 PARTS = 4
@@ -75,7 +77,7 @@ def plan(T, topo):
         p = peers[s]
         i = p.index(s)
         order.append([p[(i + o) % NS] for o in range(1, NS)])
-    helper = []
+    helper, crew = [], []
     for d in range(N):
         far = {}
         late = [s for s in peers[d] if s != d and order[s].index(d) >= NS - 1 - CALLS1[-1][1]]
@@ -85,7 +87,8 @@ def plan(T, topo):
             for s, c in zip(src, hs):
                 far[s] = (c, w)
         helper.append(far)
-    return cores, peers, partner, slc, order, helper
+        crew.append(hs)
+    return cores, peers, partner, slc, order, helper, crew
 
 
 def send(topo, src_core, dst_core, mask, sem, src, dst):
@@ -93,32 +96,69 @@ def send(topo, src_core, dst_core, mask, sem, src, dst):
     return RemoteDMATransfer(dst_ids=[DstId(rid=rid, pnc=pid)], dma_engine_mask=mask, remote_sem=sem, src=src, dst=dst)
 
 
-def helper_program(g, core, r, jobs, T, topo, cores, partner, order):
+def make_table(g, T, name, r, m, mine):
+    S, V = T.sem, g.vector
+    if name == "sel":
+        g.iota(T.si[:], [[1, 128]], 0, -16).then_inc(S.gi, 1)
+        V.wait_ge(S.gi, 1)
+        V.tensor_scalar(T.sh[:], T.si[:], 4, None, O.arith_shift_right).then_inc(S.vl, 1)
+        V.wait_ge(S.vl, 1)
+        V.tensor_scalar(T.sel[:], T.sh[:], 0, None, O.is_equal).then_inc(S.vl, 1)
+        g.wait_ge(S.vl, 2)
+        return
+    g.iota(T.pcol[:, 0:1], [[1, 1]], 0, 1).then_inc(S.gi, 1)
+    made = 2
+    if name == "t1":
+        up = NS - 1 - mine.index(r)
+        if up:
+            g.iota(T.raw[:, 0:8 * up], [[W, up], [-16, 8]], W * (r + 1) + W - 1 - C * m, 0).then_inc(S.gi, 1)
+            made += 1
+        g.iota(T.raw[:, 8 * up:64], [[W, NS - up], [-16, 8]], W * mine[0] + W - 1 - C * m, 0).then_inc(S.gi, 1)
+    elif name == "tc":
+        g.iota(T.raw[:], [[0, 8], [16, 8]], 0, 0).then_inc(S.gi, 1)
+    else:
+        g.iota(T.raw[:], [[16, 64]], 0, 0).then_inc(S.gi, 1)
+    V.wait_ge(S.gi, made)
+    V.tensor_scalar(T.rc[:, 0:1], T.pcol[:, 0:1], 15, None, O.bitwise_and).then_inc(S.vl, 1)
+    V.wait_ge(S.vl, 1)
+    V.tensor_copy(T.rf[:, 0:1], T.rc[:, 0:1]).then_inc(S.vl, 1)
+    V.wait_ge(S.vl, 2)
+    V.tensor_scalar(T[name][:], T.raw[:], T.rf[:, 0:1], None, O.subtract if name == "t1" else O.add).then_inc(S.vl, 1)
+    g.wait_ge(S.vl, 3)
+
+
+def helper_program(g, core, r, jobs, T, topo, cores, peers, partner, slc, order, crew):
+    S = T.sem
     far, near = cores[partner[r]], cores[r]
     m_far = topo.mask(core, far)
     m_near = topo.mask(core, near) & ~m_far
+    e_far, e_near = spread(m_far, NA), spread(m_near, NB)
+    name = TABLES[crew[r].index(core)]
+    make_table(g, T, name, r, slc[r], peers[r])
+    rid, pid = topo.addr(near, core)
+    g.remote_dma(T[name][:], T[name][:], S.cst, S.snt, pid, rid, e_far | e_near)
     for w, s in jobs:
         slot = T.ring[:, s * C:(s + 1) * C]
-        g.wait_ge(T.sem["arr%d" % w], engines1(order[s].index(r)))
+        g.wait_ge(S["arr%d" % w], engines1(order[s].index(r)))
         g.remote_dma_fused([
-            send(topo, core, far, spread(m_far, NA), T.sem.ringed, T.stage[w], slot),
-            send(topo, core, near, spread(m_near, NB), T.sem.ringed, T.stage[w], slot),
-        ], local_sem=T.sem.snt)
-    g.wait_ge(T.sem.snt, (NA + NB) * len(jobs))
+            send(topo, core, far, e_far, S.ringed, T.stage[w], slot),
+            send(topo, core, near, e_near, S.ringed, T.stage[w], slot),
+        ], local_sem=S.snt)
+    g.wait_ge(S.snt, (NA + NB) * (len(jobs) + 1))
 
 
 def rank_program(g, core, T, topo):
-    cores, peers, partner, slc, order, helper = plan(T, topo)
+    cores, peers, partner, slc, order, helper, crew = plan(T, topo)
     r = T.rank_of(core)
     if r is None:
         for q in range(N):
             jobs = sorted((helper[q][s][1], s) for s in helper[q] if helper[q][s][0] == core)
             if jobs:
-                helper_program(g, core, q, jobs, T, topo, cores, partner, order)
+                helper_program(g, core, q, jobs, T, topo, cores, peers, partner, slc, order, crew)
         return
     S = T.sem
     V, A = g.vector, g.scalar
-    m, mine, dests = slc[r], peers[r], order[r]
+    m, dests = slc[r], order[r]
     own_slot = T.ring[:, r * C:(r + 1) * C]
     calls = []
     k = 0
@@ -132,18 +172,8 @@ def rank_program(g, core, T, topo):
             out = own_slot if d == r else T.xs[slc[d]]
             (g.sync, A)[k % 2].dma_start(out, T.x[:, C * slc[d]:C * slc[d] + C]).then_inc(S["ld%d" % j], 16)
             k += 1
-    g.sync.dma_start(T.hhs[0:16, 0:2], T.hh[:]).then_inc(S.hl, 16)
-
-    d0 = mine[0]
-    g.iota(T.pcol[:, 0:1], [[1, 1]], 0, 1).then_inc(S.gi, 1)
-    g.iota(T.si[0:16, :], [[1, 128]], 0, -16).then_inc(S.gi, 1)
-    g.iota(T.ic[:], [[0, 8], [16, 8]], 0, 0).then_inc(S.gi, 1)
-    up = NS - 1 - mine.index(r)
-    if up:
-        g.iota(T.ib1[:, 0:8 * up], [[W, up], [-16, 8]], W * (r + 1) + W - 1 - C * m, 0).then_inc(S.gi, 1)
-    g.iota(T.ib1[:, 8 * up:64], [[W, NS - up], [-16, 8]], W * d0 + W - 1 - C * m, 0).then_inc(S.gi, 1)
-    g.iota(T.ib2[:], [[16, 64]], 0, 0).then_inc(S.gi, 1)
-    made = 6 if up else 5
+        if j == 0:
+            g.sync.dma_start(T.hhs[0:16, 0:2], T.hh[:]).then_inc(S.hl, 16)
 
     far = cores[partner[r]]
     own_engines = [eng for ds, eng in calls if r in ds][0]
@@ -169,23 +199,19 @@ def rank_program(g, core, T, topo):
         n[0] += len(instructions)
         V.wait_ge(S.vl, n[0])
 
-    O = AluOpType
-    V.wait_ge(S.gi, made)
-    step(V.tensor_scalar(T.rc[:, 0:1], T.pcol[:, 0:1], 15, None, O.bitwise_and),
-         V.tensor_scalar(T.sh[0:16, :], T.si[0:16, :], 4, None, O.arith_shift_right))
-    step(V.tensor_copy(T.rf[:, 0:1], T.rc[:, 0:1]),
-         V.tensor_scalar(T.sel[0:16, :], T.sh[0:16, :], 0, None, O.is_equal))
-    step(V.tensor_scalar(T.cc[:], T.ic[:], T.rf[:, 0:1], None, O.add))
+    tabled = (NA + NB) * len(TABLES)
     V.wait_ge(S.hl, 16)
     step(V.tensor_copy(T.hf[0:16, 0:2], T.hhs[0:16, 0:2]))
     g.tensor.wait_ge(S.vl, n[0])
+    g.tensor.wait_ge(S.cst, tabled)
     g.tensor.matmul(T.hp[:, 0:1], T.sel[0:16, :], T.hf[0:16, 0:1], True, True).then_inc(S.mm, 1)
+    V.wait_ge(S.cst, tabled)
     V.wait_ge(S.mm, 1)
-    step(V.tensor_scalar(T.a1[:], T.ib1[:], T.hp[:, 0:1], T.rf[:, 0:1], O.add, O.subtract),
-         V.tensor_scalar(T.a2[:], T.ib2[:], T.hp[:, 0:1], T.rf[:, 0:1], O.add, O.add))
+    step(V.tensor_scalar(T.a1[:], T.t1[:], T.hp[:, 0:1], None, O.add),
+         V.tensor_scalar(T.a2[:], T.t2[:], T.hp[:, 0:1], None, O.add))
     step(V.tensor_scalar(T.b1[:], T.a1[:], 3, (N - 1) * C, O.arith_shift_right, O.bitwise_and),
          V.tensor_scalar(T.b2[:], T.a2[:], W - 1, None, O.bitwise_and))
-    step(V.tensor_tensor(T.d1[:], T.b1[:], T.cc[:], O.add),
+    step(V.tensor_tensor(T.d1[:], T.b1[:], T.tc[:], O.add),
          V.tensor_copy(T.off2[:], T.b2[:]))
     step(V.tensor_copy(T.off1[:], T.d1[:]))
     listed = n[0]

@@ -7,7 +7,7 @@ O = AluOpType
 
 SCRATCH = {
     "xs": ("dram", [NS, 128, C], "bfloat16"),
-    "stage": ("dram", [2, 128, C], "bfloat16"),
+    "stage": ("dram", [3, 128, C], "bfloat16"),
     "ring": ("sbuf", [128, N * C], "bfloat16"),
     "po": ("sbuf", [128, W], "bfloat16"),
     "v": ("sbuf", [128, W], "bfloat16"),
@@ -33,30 +33,19 @@ SCRATCH = {
     "off2": ("sbuf", [128, 64], "uint16"),
     "hp": ("psum", [128, 8], "float32"),
 }
-SEMAPHORES = ["ld0", "ld1", "ld2", "hl", "gi", "vl", "mm", "arr0", "arr1", "ringed", "cst", "c0", "c1", "own", "vin",
-              "r0", "r1", "r2", "r3", "st", "snt"]
+SEMAPHORES = ["ld0", "ld1", "ld2", "ldo", "hl", "gi", "vl", "mm", "arr0", "arr1", "arr2", "ringed", "cst", "c0", "c1", "c2",
+              "own", "vin", "r0", "r1", "r2", "r3", "st", "snt"]
 
-NA, NB = 4, 4
+NR = 8
 TABLES = ["t1", "sel", "tc", "t2"]
-CALLS1 = [(False, 4, 2), (True, 3, 2)]
-CALLS3 = [(4, 2), (3, 2)]
-PARTS = 4
+WAVES = [[(0, 2), (2, 2)], [(4, 2), (6, 2)], [(0, 2), (2, 2), (4, 4)]]
+CREW = [[0, 1], [2, 3], [0, 1, 2]]
+CALLS3 = [(2, 4), (4, 2), (1, 8)]
+CUTS = [0, 320, 640, 832, 1024]
 
 
 def bits(mask):
     return [1 << b for b in range(16) if mask >> b & 1]
-
-
-def spread(mask, n):
-    b = bits(mask)
-    return sum(b[::len(b) // n][:n])
-
-
-def engines1(k):
-    for own, n, e in CALLS1:
-        if k < n:
-            return e
-        k -= n
 
 
 def plan(T, topo):
@@ -79,13 +68,14 @@ def plan(T, topo):
         order.append([p[(i + o) % NS] for o in range(1, NS)])
     helper, crew = [], []
     for d in range(N):
-        far = {}
-        late = [s for s in peers[d] if s != d and order[s].index(d) >= NS - 1 - CALLS1[-1][1]]
-        first = [s for s in peers[d] if s != d and s not in late]
         hs = sorted(mates[d][::2], key=lambda c: -abs(c - cores[d]))
-        for w, src in ((0, first), (1, late)):
-            for s, c in zip(src, hs):
-                far[s] = (c, w)
+        far = {}
+        k = 0
+        for w, engs in enumerate(WAVES):
+            for h, (at, cnt) in zip(CREW[w], engs):
+                s = [s for s in peers[d] if s != d and order[s][k] == d][0]
+                far[s] = (hs[h], w, cnt)
+                k += 1
         helper.append(far)
         crew.append(hs)
     return cores, peers, partner, slc, order, helper, crew
@@ -127,24 +117,24 @@ def make_table(g, T, name, r, m, mine):
     g.wait_ge(S.vl, 3)
 
 
-def helper_program(g, core, r, jobs, T, topo, cores, peers, partner, slc, order, crew):
+def helper_program(g, core, r, jobs, T, topo, cores, peers, partner, slc, crew):
     S = T.sem
     far, near = cores[partner[r]], cores[r]
     m_far = topo.mask(core, far)
-    m_near = topo.mask(core, near) & ~m_far
-    e_far, e_near = spread(m_far, NA), spread(m_near, NB)
+    e_far = sum(bits(m_far)[:NR])
+    e_near = sum(bits(topo.mask(core, near) & ~m_far)[:NR])
     name = TABLES[crew[r].index(core)]
     make_table(g, T, name, r, slc[r], peers[r])
     rid, pid = topo.addr(near, core)
     g.remote_dma(T[name][:], T[name][:], S.cst, S.snt, pid, rid, e_far | e_near)
-    for w, s in jobs:
+    for w, s, cnt in jobs:
         slot = T.ring[:, s * C:(s + 1) * C]
-        g.wait_ge(S["arr%d" % w], engines1(order[s].index(r)))
+        g.wait_ge(S["arr%d" % w], cnt)
         g.remote_dma_fused([
             send(topo, core, far, e_far, S.ringed, T.stage[w], slot),
             send(topo, core, near, e_near, S.ringed, T.stage[w], slot),
         ], local_sem=S.snt)
-    g.wait_ge(S.snt, (NA + NB) * (len(jobs) + 1))
+    g.wait_ge(S.snt, 2 * NR * (len(jobs) + 1))
 
 
 def rank_program(g, core, T, topo):
@@ -152,44 +142,41 @@ def rank_program(g, core, T, topo):
     r = T.rank_of(core)
     if r is None:
         for q in range(N):
-            jobs = sorted((helper[q][s][1], s) for s in helper[q] if helper[q][s][0] == core)
+            jobs = sorted((w, s, cnt) for s, (c, w, cnt) in helper[q].items() if c == core)
             if jobs:
-                helper_program(g, core, q, jobs, T, topo, cores, peers, partner, slc, order, crew)
+                helper_program(g, core, q, jobs, T, topo, cores, peers, partner, slc, crew)
         return
     S = T.sem
     V, A = g.vector, g.scalar
     m, dests = slc[r], order[r]
     own_slot = T.ring[:, r * C:(r + 1) * C]
-    calls = []
-    k = 0
-    for own, cnt, eng in CALLS1:
-        calls.append((dests[k:k + cnt] + ([r] if own else []), eng))
-        k += cnt
 
     k = 0
-    for j, (ds, eng) in enumerate(calls):
-        for d in ds:
-            out = own_slot if d == r else T.xs[slc[d]]
-            (g.sync, A)[k % 2].dma_start(out, T.x[:, C * slc[d]:C * slc[d] + C]).then_inc(S["ld%d" % j], 16)
+    for j, engs in enumerate(WAVES):
+        for _ in engs:
+            d = dests[k]
+            (g.sync, A)[k % 2].dma_start(T.xs[slc[d]], T.x[:, C * slc[d]:C * slc[d] + C]).then_inc(S["ld%d" % j], 16)
             k += 1
-        if j == 0:
-            g.sync.dma_start(T.hhs[0:16, 0:2], T.hh[:]).then_inc(S.hl, 16)
+    A.dma_start(own_slot, T.x[:, C * m:C * m + C]).then_inc(S.ldo, 16)
+    g.sync.dma_start(T.hhs[0:16, 0:2], T.hh[:]).then_inc(S.hl, 16)
 
-    far = cores[partner[r]]
-    own_engines = [eng for ds, eng in calls if r in ds][0]
     sent = 0
-    for j, (ds, eng) in enumerate(calls):
-        g.wait_ge(S["ld%d" % j], 16 * len(ds))
+    k = 0
+    for j, engs in enumerate(WAVES):
+        g.wait_ge(S["ld%d" % j], 16 * len(engs))
         tr = []
-        for d in ds:
-            c, hw = (far, None) if d == r else helper[d][r]
-            b = bits(topo.mask(core, c))[eng * len(tr):eng * len(tr) + eng]
-            if d == r:
-                tr.append(send(topo, core, c, sum(b), S.ringed, own_slot, own_slot))
-            else:
-                tr.append(send(topo, core, c, sum(b), S["arr%d" % hw], T.xs[slc[d]], T.stage[hw]))
+        for at, cnt in engs:
+            d = dests[k]
+            c = helper[d][r][0]
+            tr.append(send(topo, core, c, sum(bits(topo.mask(core, c))[at:at + cnt]), S["arr%d" % j], T.xs[slc[d]], T.stage[j]))
+            sent += cnt
+            k += 1
         g.remote_dma_fused(tr, local_sem=S.snt)
-        sent += eng * len(tr)
+    far = cores[partner[r]]
+    rid, pid = topo.addr(far, core)
+    g.wait_ge(S.ldo, 16)
+    g.remote_dma(own_slot, own_slot, S.ringed, S.snt, pid, rid, sum(bits(topo.mask(core, far))[:NR]))
+    sent += NR
 
     n = [0]
 
@@ -199,7 +186,7 @@ def rank_program(g, core, T, topo):
         n[0] += len(instructions)
         V.wait_ge(S.vl, n[0])
 
-    tabled = (NA + NB) * len(TABLES)
+    tabled = 2 * NR * len(TABLES)
     V.wait_ge(S.hl, 16)
     step(V.tensor_copy(T.hf[0:16, 0:2], T.hhs[0:16, 0:2]))
     g.tensor.wait_ge(S.vl, n[0])
@@ -224,10 +211,9 @@ def rank_program(g, core, T, topo):
     def by_a(out, win, off, a, b):
         return A.activation(out, win.indirect(off[:, a // 16:b // 16]), copy, bias=-0.0)
 
-    own_load = [j for j, (ds, eng) in enumerate(calls) if r in ds][0]
     for q in (V, A):
-        q.wait_ge(S["ld%d" % own_load], 16 * len(calls[own_load][0]))
-        q.wait_ge(S.ringed, len(dests) * (NA + NB) + own_engines)
+        q.wait_ge(S.ldo, 16)
+        q.wait_ge(S.ringed, NR * (N - 1))
     A.wait_ge(S.vl, listed)
     ring = T.ring[:, 0:N * C]
     lo = 0
@@ -254,14 +240,13 @@ def rank_program(g, core, T, topo):
     for q in (V, A):
         q.wait_ge(S.own, 1)
         q.wait_ge(S.vin, got)
-    Q = W // PARTS
     v = T.v[:, 0:W]
-    for k in range(PARTS):
-        a, b = k * Q, (k + 1) * Q
+    parts = list(zip(CUTS, CUTS[1:]))
+    for k, (a, b) in enumerate(parts):
         (by_v, by_a)[k % 2](T.yb[:, a:b], v, T.off2, a, b).then_inc(S["r%d" % k], 1)
-    for k in range(PARTS):
-        q = A if k == PARTS - 1 else g.sync
+    for k, (a, b) in enumerate(parts):
+        q = A if k == len(parts) - 1 else g.sync
         q.wait_ge(S["r%d" % k], 1)
-        q.dma_start(T.y[:, k * Q:(k + 1) * Q], T.yb[:, k * Q:(k + 1) * Q]).then_inc(S.st, 16)
-    g.sync.wait_ge(S.st, 16 * PARTS)
+        q.dma_start(T.y[:, a:b], T.yb[:, a:b]).then_inc(S.st, 16)
+    g.sync.wait_ge(S.st, 16 * len(parts))
     g.wait_ge(S.snt, sent)

@@ -7,7 +7,8 @@ O = AluOpType
 
 SCRATCH = {
     "xs": ("dram", [NS, 128, C], "bfloat16"),
-    "stage": ("dram", [3, 128, C], "bfloat16"),
+    "stage": ("dram", [4, 128, C], "bfloat16"),
+    "fw": ("sbuf", [128, C], "bfloat16"),
     "ring": ("sbuf", [128, N * C], "bfloat16"),
     "po": ("sbuf", [128, W], "bfloat16"),
     "v": ("sbuf", [128, W], "bfloat16"),
@@ -18,6 +19,7 @@ SCRATCH = {
     "rc": ("sbuf", [128, 8], "int32"),
     "rf": ("sbuf", [128, 8], "float32"),
     "raw": ("sbuf", [128, 64], "int32"),
+    "cols": ("sbuf", [128, 64], "int32"),
     "si": ("sbuf", [128, 128], "int32"),
     "sh": ("sbuf", [128, 128], "int32"),
     "sel": ("sbuf", [128, 128], "float32"),
@@ -33,14 +35,15 @@ SCRATCH = {
     "off2": ("sbuf", [128, 64], "uint16"),
     "hp": ("psum", [128, 8], "float32"),
 }
-SEMAPHORES = ["ld0", "ld1", "ld2", "ldo", "hl", "gi", "vl", "mm", "arr0", "arr1", "arr2", "ringed", "cst", "c0", "c1", "c2",
-              "own", "vin", "r0", "r1", "r2", "r3", "st", "snt"]
+SEMAPHORES = ["ld0", "ld1", "ld2", "ld3", "ldo", "hl", "gi", "vl", "vt", "mm", "arr0", "arr1", "arr2", "arr3", "ringed", "cst",
+              "cnt", "ctt", "c0", "c1", "c2", "fwd", "own", "vin", "r0", "r1", "r2", "r3", "st", "snt"]
 
 NR = 8
-TABLES = ["t1", "sel", "tc", "t2"]
-WAVES = [[(0, 2), (2, 2)], [(4, 2), (6, 2)], [(0, 2), (2, 2), (4, 4)]]
-CREW = [[0, 1], [2, 3], [0, 1, 2]]
-CALLS3 = [(2, 4), (4, 2), (1, 8)]
+TABLES = [("t1", 0, 32), ("sel", 0, 128), ("t1", 32, 64), ("tc", 0, 64)]
+WAVES = [(True, [(0, 8, 0)]), (True, [(0, 4, 1), (4, 4, 2)]),
+         (False, [(0, 4, 0), (4, 4, 1)]), (False, [(0, 4, 2), (4, 4, 3)])]
+RELAYED = 2
+CALLS3 = [(2, 4), (1, 8), (4, 2)]
 CUTS = [0, 320, 640, 832, 1024]
 
 
@@ -56,29 +59,35 @@ def plan(T, topo):
                 and topo.may_write(cores[r], cores[s])][0] for r in range(N)]
     slc = [peers[r].index(r) if rk[r] == rk[0] else peers[0].index(partner[r]) for r in range(N)]
     where = {(topo.host(cores[r]), topo.chip(cores[r])): r for r in range(N)}
-    mates = [[] for _ in range(N)]
+    others = [[] for _ in range(N)]
     for c in range(512):
         r = where.get((topo.host(c), topo.chip(c)))
         if r is not None and c != cores[r]:
-            mates[r].append(c)
-    order = []
+            others[r].append(c)
+    order, crew = [], []
     for s in range(N):
-        p = peers[s]
-        i = p.index(s)
-        order.append([p[(i + o) % NS] for o in range(1, NS)])
-    helper, crew = [], []
-    for d in range(N):
-        hs = sorted(mates[d][::2], key=lambda c: -abs(c - cores[d]))
-        far = {}
-        k = 0
-        for w, engs in enumerate(WAVES):
-            for h, (at, cnt) in zip(CREW[w], engs):
-                s = [s for s in peers[d] if s != d and order[s][k] == d][0]
-                far[s] = (hs[h], w, cnt)
-                k += 1
-        helper.append(far)
-        crew.append(hs)
-    return cores, peers, partner, slc, order, helper, crew
+        i = peers[s].index(s)
+        order.append([peers[s][(i + o) % NS] for o in range(1, NS)])
+        crew.append(sorted(others[s][::2], key=lambda c: -abs(c - cores[s])))
+    jobs = []
+    for s in range(N):
+        both = [d for d in peers[s] if topo.may_write(cores[s], cores[partner[d]])]
+        rest = [d for d in peers[s] if d not in both]
+        i = both.index(s)
+        near = [both[(i + o) % len(both)] for o in range(1, len(both))]
+        away = [rest[(i + o) % len(rest)] for o in range(len(rest))]
+        for w, (here, engs) in enumerate(WAVES):
+            for at, cnt, h in engs:
+                d = (near if here else away).pop(0)
+                jobs.append((w, s, d, crew[s if here else d][h], at, cnt, here))
+    return cores, peers, partner, slc, order, crew, sorted(jobs)
+
+
+def ways(topo, core, near, far):
+    f, a = topo.mask(core, far), topo.mask(core, near)
+    if len(bits(a & ~f)) >= NR:
+        return bits(f)[:NR], bits(a & ~f)[:NR]
+    return bits(f)[:NR // 2], bits(f)[NR // 2:NR]
 
 
 def send(topo, src_core, dst_core, mask, sem, src, dst):
@@ -86,7 +95,7 @@ def send(topo, src_core, dst_core, mask, sem, src, dst):
     return RemoteDMATransfer(dst_ids=[DstId(rid=rid, pnc=pid)], dma_engine_mask=mask, remote_sem=sem, src=src, dst=dst)
 
 
-def make_table(g, T, name, r, m, mine):
+def make_table(g, T, name, lo, hi, r, m, mine):
     S, V = T.sem, g.vector
     if name == "sel":
         g.iota(T.si[:], [[1, 128]], 0, -16).then_inc(S.gi, 1)
@@ -97,80 +106,101 @@ def make_table(g, T, name, r, m, mine):
         g.wait_ge(S.vl, 2)
         return
     g.iota(T.pcol[:, 0:1], [[1, 1]], 0, 1).then_inc(S.gi, 1)
-    made = 2
+    made = 1
     if name == "t1":
         up = NS - 1 - mine.index(r)
-        if up:
-            g.iota(T.raw[:, 0:8 * up], [[W, up], [-16, 8]], W * (r + 1) + W - 1 - C * m, 0).then_inc(S.gi, 1)
-            made += 1
-        g.iota(T.raw[:, 8 * up:64], [[W, NS - up], [-16, 8]], W * mine[0] + W - 1 - C * m, 0).then_inc(S.gi, 1)
-    elif name == "tc":
-        g.iota(T.raw[:], [[0, 8], [16, 8]], 0, 0).then_inc(S.gi, 1)
+        for a, b, first in ((0, up, r + 1), (up, NS, mine[0])):
+            s, e = max(a, lo // 8), min(b, hi // 8)
+            if s < e:
+                g.iota(T.raw[:, 8 * s:8 * e], [[W, e - s], [-16, 8]], W * (first + s - a) + W - 1 - C * m, 0).then_inc(S.gi, 1)
+                made += 1
     else:
-        g.iota(T.raw[:], [[16, 64]], 0, 0).then_inc(S.gi, 1)
+        g.iota(T.raw[:], [[0, 8], [16, 8]], 0, 0).then_inc(S.gi, 1)
+        made += 1
     V.wait_ge(S.gi, made)
     V.tensor_scalar(T.rc[:, 0:1], T.pcol[:, 0:1], 15, None, O.bitwise_and).then_inc(S.vl, 1)
     V.wait_ge(S.vl, 1)
     V.tensor_copy(T.rf[:, 0:1], T.rc[:, 0:1]).then_inc(S.vl, 1)
     V.wait_ge(S.vl, 2)
-    V.tensor_scalar(T[name][:], T.raw[:], T.rf[:, 0:1], None, O.subtract if name == "t1" else O.add).then_inc(S.vl, 1)
+    V.tensor_scalar(T[name][:, lo:hi], T.raw[:, lo:hi], T.rf[:, 0:1], None,
+                    O.subtract if name == "t1" else O.add).then_inc(S.vl, 1)
     g.wait_ge(S.vl, 3)
 
 
-def helper_program(g, core, r, jobs, T, topo, cores, peers, partner, slc, crew):
-    S = T.sem
-    far, near = cores[partner[r]], cores[r]
-    m_far = topo.mask(core, far)
-    e_far = sum(bits(m_far)[:NR])
-    e_near = sum(bits(topo.mask(core, near) & ~m_far)[:NR])
-    name = TABLES[crew[r].index(core)]
-    make_table(g, T, name, r, slc[r], peers[r])
-    rid, pid = topo.addr(near, core)
-    g.remote_dma(T[name][:], T[name][:], S.cst, S.snt, pid, rid, e_far | e_near)
-    for w, s, cnt in jobs:
+def helper_program(g, core, r, T, topo, cores, peers, partner, slc, order, crew, jobs):
+    S, V = T.sem, g.vector
+    at = crew[r].index(core)
+    name, lo, hi = TABLES[at]
+    make_table(g, T, name, lo, hi, r, slc[r], peers[r])
+    rid, pid = topo.addr(cores[r], core)
+    f, a = ways(topo, core, cores[r], cores[partner[r]])
+    g.remote_dma(T[name][:, lo:hi], T[name][:, lo:hi], S.cst, S.snt, pid, rid, sum(f + a))
+    sent = len(f + a)
+    for w, s, d, c, _, cnt, _ in jobs:
+        if c != core:
+            continue
         slot = T.ring[:, s * C:(s + 1) * C]
+        fs, ns = ways(topo, core, cores[d], cores[partner[d]])
         g.wait_ge(S["arr%d" % w], cnt)
         g.remote_dma_fused([
-            send(topo, core, far, e_far, S.ringed, T.stage[w], slot),
-            send(topo, core, near, e_near, S.ringed, T.stage[w], slot),
+            send(topo, core, cores[partner[d]], sum(fs), S.ringed, T.stage[w], slot),
+            send(topo, core, cores[d], sum(ns), S.ringed, T.stage[w], slot),
         ], local_sem=S.snt)
-    g.wait_ge(S.snt, 2 * NR * (len(jobs) + 1))
+        sent += len(fs + ns)
+    if at == len(TABLES) - 1:
+        V.wait_ge(S.cnt, 2 * NR)
+        V.tensor_scalar(T.t2[:], T.cols[:], T.rf[:, 0:1], None, O.add).then_inc(S.vt, 1)
+        g.wait_ge(S.vt, 1)
+        g.remote_dma(T.t2[:], T.t2[:], S.ctt, S.snt, pid, rid, sum(f + a))
+        sent += len(f + a)
+    if at < RELAYED:
+        m, d = slc[r], cores[order[r][at]]
+        rid, pid = topo.addr(d, core)
+        g.wait_ge(S.fwd, CALLS3[0][1])
+        g.remote_dma(T.v[:, m * C:(m + 1) * C], T.fw[:], S.vin, S.snt, pid, rid, sum(bits(topo.mask(core, d))[:NR]))
+        sent += NR
+    g.wait_ge(S.snt, sent)
 
 
 def rank_program(g, core, T, topo):
-    cores, peers, partner, slc, order, helper, crew = plan(T, topo)
+    cores, peers, partner, slc, order, crew, jobs = plan(T, topo)
     r = T.rank_of(core)
     if r is None:
         for q in range(N):
-            jobs = sorted((w, s, cnt) for s, (c, w, cnt) in helper[q].items() if c == core)
-            if jobs:
-                helper_program(g, core, q, jobs, T, topo, cores, peers, partner, slc, crew)
+            if core in crew[q]:
+                helper_program(g, core, q, T, topo, cores, peers, partner, slc, order, crew, jobs)
         return
     S = T.sem
     V, A = g.vector, g.scalar
     m, dests = slc[r], order[r]
     own_slot = T.ring[:, r * C:(r + 1) * C]
+    mine = [[j for j in jobs if j[0] == w and j[1] == r] for w in range(len(WAVES))]
+    mine = [sorted(js, key=lambda j: j[4]) for js in mine]
+    off_chip = topo.mask(core, cores[dests[0]])
 
     k = 0
-    for j, engs in enumerate(WAVES):
-        for _ in engs:
-            d = dests[k]
-            (g.sync, A)[k % 2].dma_start(T.xs[slc[d]], T.x[:, C * slc[d]:C * slc[d] + C]).then_inc(S["ld%d" % j], 16)
+    for w, js in enumerate(mine):
+        for j in js:
+            t = slc[j[2]]
+            (g.sync, A)[k % 2].dma_start(T.xs[t], T.x[:, C * t:C * t + C]).then_inc(S["ld%d" % w], 16)
             k += 1
+            if k == 1:
+                g.sync.dma_start(T.hhs[0:16, 0:2], T.hh[:]).then_inc(S.hl, 16)
     A.dma_start(own_slot, T.x[:, C * m:C * m + C]).then_inc(S.ldo, 16)
-    g.sync.dma_start(T.hhs[0:16, 0:2], T.hh[:]).then_inc(S.hl, 16)
 
-    sent = 0
-    k = 0
-    for j, engs in enumerate(WAVES):
-        g.wait_ge(S["ld%d" % j], 16 * len(engs))
+    g.iota(T.raw[:], [[16, 64]], 0, 0).then_inc(S.gi, 1)
+    g.wait_ge(S.gi, 1)
+    rid, pid = topo.addr(crew[r][-1], core)
+    g.remote_dma(T.cols[:], T.raw[:], S.cnt, S.snt, pid, rid, sum(bits(topo.mask(core, crew[r][-1]))[:2 * NR]))
+    sent = 2 * NR
+
+    for w, js in enumerate(mine):
+        g.wait_ge(S["ld%d" % w], 16 * len(js))
         tr = []
-        for at, cnt in engs:
-            d = dests[k]
-            c = helper[d][r][0]
-            tr.append(send(topo, core, c, sum(bits(topo.mask(core, c))[at:at + cnt]), S["arr%d" % j], T.xs[slc[d]], T.stage[j]))
+        for _, _, d, c, at, cnt, here in js:
+            e = bits(topo.mask(core, c) & ~off_chip) if here else bits(topo.mask(core, c))
+            tr.append(send(topo, core, c, sum(e[at:at + cnt]), S["arr%d" % w], T.xs[slc[d]], T.stage[w]))
             sent += cnt
-            k += 1
         g.remote_dma_fused(tr, local_sem=S.snt)
     far = cores[partner[r]]
     rid, pid = topo.addr(far, core)
@@ -178,30 +208,21 @@ def rank_program(g, core, T, topo):
     g.remote_dma(own_slot, own_slot, S.ringed, S.snt, pid, rid, sum(bits(topo.mask(core, far))[:NR]))
     sent += NR
 
-    n = [0]
-
-    def step(*instructions):
-        for ins in instructions:
-            ins.then_inc(S.vl, 1)
-        n[0] += len(instructions)
-        V.wait_ge(S.vl, n[0])
-
     tabled = 2 * NR * len(TABLES)
     V.wait_ge(S.hl, 16)
-    step(V.tensor_copy(T.hf[0:16, 0:2], T.hhs[0:16, 0:2]))
-    g.tensor.wait_ge(S.vl, n[0])
+    V.tensor_copy(T.hf[0:16, 0:1], T.hhs[0:16, 0:1]).then_inc(S.vl, 1)
     g.tensor.wait_ge(S.cst, tabled)
+    g.tensor.wait_ge(S.vl, 1)
     g.tensor.matmul(T.hp[:, 0:1], T.sel[0:16, :], T.hf[0:16, 0:1], True, True).then_inc(S.mm, 1)
     V.wait_ge(S.cst, tabled)
     V.wait_ge(S.mm, 1)
-    step(V.tensor_scalar(T.a1[:], T.t1[:], T.hp[:, 0:1], None, O.add),
-         V.tensor_scalar(T.a2[:], T.t2[:], T.hp[:, 0:1], None, O.add))
-    step(V.tensor_scalar(T.b1[:], T.a1[:], 3, (N - 1) * C, O.arith_shift_right, O.bitwise_and),
-         V.tensor_scalar(T.b2[:], T.a2[:], W - 1, None, O.bitwise_and))
-    step(V.tensor_tensor(T.d1[:], T.b1[:], T.tc[:], O.add),
-         V.tensor_copy(T.off2[:], T.b2[:]))
-    step(V.tensor_copy(T.off1[:], T.d1[:]))
-    listed = n[0]
+    V.tensor_scalar(T.a1[:], T.t1[:], T.hp[:, 0:1], None, O.add).then_inc(S.vl, 1)
+    V.wait_ge(S.vl, 2)
+    V.tensor_scalar(T.b1[:], T.a1[:], 3, (N - 1) * C, O.arith_shift_right, O.bitwise_and).then_inc(S.vl, 1)
+    V.wait_ge(S.vl, 3)
+    V.tensor_tensor(T.d1[:], T.b1[:], T.tc[:], O.add).then_inc(S.vl, 1)
+    V.wait_ge(S.vl, 4)
+    V.tensor_copy(T.off1[:], T.d1[:]).then_inc(S.vl, 1)
 
     copy = ActivationFunctionType.Copy
 
@@ -211,10 +232,15 @@ def rank_program(g, core, T, topo):
     def by_a(out, win, off, a, b):
         return A.activation(out, win.indirect(off[:, a // 16:b // 16]), copy, bias=-0.0)
 
+    filled = NR
+    for _, _, d, c, _, _, _ in jobs:
+        if r in (d, partner[d]):
+            f, a = ways(topo, c, cores[d], cores[partner[d]])
+            filled += len(a) if d == r else len(f)
     for q in (V, A):
+        q.wait_ge(S.vl, 5)
         q.wait_ge(S.ldo, 16)
-        q.wait_ge(S.ringed, NR * (N - 1))
-    A.wait_ge(S.vl, listed)
+        q.wait_ge(S.ringed, filled)
     ring = T.ring[:, 0:N * C]
     lo = 0
     for j, (cnt, eng) in enumerate(CALLS3):
@@ -229,15 +255,31 @@ def rank_program(g, core, T, topo):
     for j, (cnt, eng) in enumerate(CALLS3):
         g.wait_ge(S["c%d" % j], 2)
         tr = []
-        for d in dests[e:e + cnt]:
-            b = bits(topo.mask(core, cores[d]))[eng * len(tr):eng * len(tr) + eng]
-            tr.append(send(topo, core, cores[d], sum(b), S.vin, T.po[:, e * C:(e + 1) * C], T.v[:, m * C:(m + 1) * C]))
+        for _ in range(cnt):
+            piece = T.po[:, e * C:(e + 1) * C]
+            at = eng * len(tr)
+            if e < RELAYED:
+                c = crew[r][e]
+                b = bits(topo.mask(core, c) & ~off_chip)[at:at + eng]
+                tr.append(send(topo, core, c, sum(b), S.fwd, piece, T.fw[:]))
+            else:
+                c = cores[dests[e]]
+                b = bits(topo.mask(core, c))[at:at + eng]
+                tr.append(send(topo, core, c, sum(b), S.vin, piece, T.v[:, m * C:(m + 1) * C]))
             e += 1
         g.remote_dma_fused(tr, local_sem=S.snt)
         sent += eng * cnt
 
-    got = sum(cnt * eng for cnt, eng in CALLS3)
+    V.wait_ge(S.ctt, 2 * NR)
+    V.tensor_scalar(T.a2[:], T.t2[:], T.hp[:, 0:1], None, O.add).then_inc(S.vt, 1)
+    V.wait_ge(S.vt, 1)
+    V.tensor_scalar(T.b2[:], T.a2[:], W - 1, None, O.bitwise_and).then_inc(S.vt, 1)
+    V.wait_ge(S.vt, 2)
+    V.tensor_copy(T.off2[:], T.b2[:]).then_inc(S.vt, 1)
+
+    got = NR * RELAYED + sum(cnt * eng for cnt, eng in CALLS3[1:])
     for q in (V, A):
+        q.wait_ge(S.vt, 3)
         q.wait_ge(S.own, 1)
         q.wait_ge(S.vin, got)
     v = T.v[:, 0:W]

from concourse.bass import DstId, RemoteDMATransfer
from concourse.mybir import AluOpType, ActivationFunctionType

N, W, C = 16, 1024, 128
NS = W // C
O = AluOpType

SCRATCH = {
    "xs": ("dram", [NS, 128, C], "bfloat16"),
    "stage": ("dram", [4, 128, C], "bfloat16"),
    "fw": ("sbuf", [128, C], "bfloat16"),
    "ring": ("sbuf", [128, N * C], "bfloat16"),
    "po": ("sbuf", [128, W], "bfloat16"),
    "v": ("sbuf", [128, W], "bfloat16"),
    "yb": ("sbuf", [128, W], "bfloat16"),
    "hhs": ("sbuf", [128, 8], "int32"),
    "hf": ("sbuf", [128, 8], "float32"),
    "pcol": ("sbuf", [128, 8], "int32"),
    "rc": ("sbuf", [128, 8], "int32"),
    "rf": ("sbuf", [128, 8], "float32"),
    "raw": ("sbuf", [128, 64], "int32"),
    "cols": ("sbuf", [128, 64], "int32"),
    "si": ("sbuf", [128, 128], "int32"),
    "sh": ("sbuf", [128, 128], "int32"),
    "sel": ("sbuf", [128, 128], "float32"),
    "t1": ("sbuf", [128, 64], "int32"),
    "tc": ("sbuf", [128, 64], "int32"),
    "t2": ("sbuf", [128, 64], "int32"),
    "a1": ("sbuf", [128, 64], "int32"),
    "b1": ("sbuf", [128, 64], "int32"),
    "d1": ("sbuf", [128, 64], "int32"),
    "a2": ("sbuf", [128, 64], "int32"),
    "b2": ("sbuf", [128, 64], "int32"),
    "off1": ("sbuf", [128, 64], "uint16"),
    "off2": ("sbuf", [128, 64], "uint16"),
    "hp": ("psum", [128, 8], "float32"),
}
SEMAPHORES = ["ld0", "ld1", "ld2", "ld3", "ldo", "hl", "gi", "vl", "vt", "mm", "arr0", "arr1", "arr2", "arr3", "ringed", "cst",
              "cnt", "ctt", "c0", "c1", "c2", "fwd", "own", "vin", "r0", "r1", "r2", "r3", "st", "snt"]

NR = 8
TABLES = [("t1", 0, 32), ("sel", 0, 128), ("t1", 32, 64), ("tc", 0, 64)]
WAVES = [(True, [(0, 8, 0)]), (True, [(0, 4, 1), (4, 4, 2)]),
         (False, [(0, 4, 0), (4, 4, 1)]), (False, [(0, 4, 2), (4, 4, 3)])]
RELAYED = 2
CALLS3 = [(2, 4), (1, 8), (4, 2)]
CUTS = [0, 320, 640, 832, 1024]


def bits(mask):
    return [1 << b for b in range(16) if mask >> b & 1]


def plan(T, topo):
    cores = [int(c) for c in T.cores]
    rk = [topo.rack(topo.host(c)) for c in cores]
    peers = [[s for s in range(N) if rk[s] == rk[r]] for r in range(N)]
    partner = [[s for s in range(N) if rk[s] != rk[r] and topo.chip(cores[s]) == topo.chip(cores[r])
                and topo.may_write(cores[r], cores[s])][0] for r in range(N)]
    slc = [peers[r].index(r) if rk[r] == rk[0] else peers[0].index(partner[r]) for r in range(N)]
    where = {(topo.host(cores[r]), topo.chip(cores[r])): r for r in range(N)}
    others = [[] for _ in range(N)]
    for c in range(512):
        r = where.get((topo.host(c), topo.chip(c)))
        if r is not None and c != cores[r]:
            others[r].append(c)
    order, crew = [], []
    for s in range(N):
        i = peers[s].index(s)
        order.append([peers[s][(i + o) % NS] for o in range(1, NS)])
        crew.append(sorted(others[s][::2], key=lambda c: -abs(c - cores[s])))
    jobs = []
    for s in range(N):
        both = [d for d in peers[s] if topo.may_write(cores[s], cores[partner[d]])]
        rest = [d for d in peers[s] if d not in both]
        i = both.index(s)
        near = [both[(i + o) % len(both)] for o in range(1, len(both))]
        away = [rest[(i + o) % len(rest)] for o in range(len(rest))]
        for w, (here, engs) in enumerate(WAVES):
            for at, cnt, h in engs:
                d = (near if here else away).pop(0)
                jobs.append((w, s, d, crew[s if here else d][h], at, cnt, here))
    return cores, peers, partner, slc, order, crew, sorted(jobs)


def ways(topo, core, near, far):
    f, a = topo.mask(core, far), topo.mask(core, near)
    if len(bits(a & ~f)) >= NR:
        return bits(f)[:NR], bits(a & ~f)[:NR]
    return bits(f)[:NR // 2], bits(f)[NR // 2:NR]


def send(topo, src_core, dst_core, mask, sem, src, dst):
    rid, pid = topo.addr(dst_core, src_core)
    return RemoteDMATransfer(dst_ids=[DstId(rid=rid, pnc=pid)], dma_engine_mask=mask, remote_sem=sem, src=src, dst=dst)


def make_table(g, T, name, lo, hi, r, m, mine):
    S, V = T.sem, g.vector
    if name == "sel":
        g.iota(T.si[:], [[1, 128]], 0, -16).then_inc(S.gi, 1)
        V.wait_ge(S.gi, 1)
        V.tensor_scalar(T.sh[:], T.si[:], 4, None, O.arith_shift_right).then_inc(S.vl, 1)
        V.wait_ge(S.vl, 1)
        V.tensor_scalar(T.sel[:], T.sh[:], 0, None, O.is_equal).then_inc(S.vl, 1)
        g.wait_ge(S.vl, 2)
        return
    g.iota(T.pcol[:, 0:1], [[1, 1]], 0, 1).then_inc(S.gi, 1)
    made = 1
    if name == "t1":
        up = NS - 1 - mine.index(r)
        for a, b, first in ((0, up, r + 1), (up, NS, mine[0])):
            s, e = max(a, lo // 8), min(b, hi // 8)
            if s < e:
                g.iota(T.raw[:, 8 * s:8 * e], [[W, e - s], [-16, 8]], W * (first + s - a) + W - 1 - C * m, 0).then_inc(S.gi, 1)
                made += 1
    else:
        g.iota(T.raw[:], [[0, 8], [16, 8]], 0, 0).then_inc(S.gi, 1)
        made += 1
    V.wait_ge(S.gi, made)
    V.tensor_scalar(T.rc[:, 0:1], T.pcol[:, 0:1], 15, None, O.bitwise_and).then_inc(S.vl, 1)
    V.wait_ge(S.vl, 1)
    V.tensor_copy(T.rf[:, 0:1], T.rc[:, 0:1]).then_inc(S.vl, 1)
    V.wait_ge(S.vl, 2)
    V.tensor_scalar(T[name][:, lo:hi], T.raw[:, lo:hi], T.rf[:, 0:1], None,
                    O.subtract if name == "t1" else O.add).then_inc(S.vl, 1)
    g.wait_ge(S.vl, 3)


def helper_program(g, core, r, T, topo, cores, peers, partner, slc, order, crew, jobs):
    S, V = T.sem, g.vector
    at = crew[r].index(core)
    name, lo, hi = TABLES[at]
    make_table(g, T, name, lo, hi, r, slc[r], peers[r])
    rid, pid = topo.addr(cores[r], core)
    f, a = ways(topo, core, cores[r], cores[partner[r]])
    g.remote_dma(T[name][:, lo:hi], T[name][:, lo:hi], S.cst, S.snt, pid, rid, sum(f + a))
    sent = len(f + a)
    for w, s, d, c, _, cnt, _ in jobs:
        if c != core:
            continue
        slot = T.ring[:, s * C:(s + 1) * C]
        fs, ns = ways(topo, core, cores[d], cores[partner[d]])
        g.wait_ge(S["arr%d" % w], cnt)
        g.remote_dma_fused([
            send(topo, core, cores[partner[d]], sum(fs), S.ringed, T.stage[w], slot),
            send(topo, core, cores[d], sum(ns), S.ringed, T.stage[w], slot),
        ], local_sem=S.snt)
        sent += len(fs + ns)
    if at == len(TABLES) - 1:
        V.wait_ge(S.cnt, 2 * NR)
        V.tensor_scalar(T.t2[:], T.cols[:], T.rf[:, 0:1], None, O.add).then_inc(S.vt, 1)
        g.wait_ge(S.vt, 1)
        g.remote_dma(T.t2[:], T.t2[:], S.ctt, S.snt, pid, rid, sum(f + a))
        sent += len(f + a)
    if at < RELAYED:
        m, d = slc[r], cores[order[r][at]]
        rid, pid = topo.addr(d, core)
        g.wait_ge(S.fwd, CALLS3[0][1])
        g.remote_dma(T.v[:, m * C:(m + 1) * C], T.fw[:], S.vin, S.snt, pid, rid, sum(bits(topo.mask(core, d))[:NR]))
        sent += NR
    g.wait_ge(S.snt, sent)


def rank_program(g, core, T, topo):
    cores, peers, partner, slc, order, crew, jobs = plan(T, topo)
    r = T.rank_of(core)
    if r is None:
        for q in range(N):
            if core in crew[q]:
                helper_program(g, core, q, T, topo, cores, peers, partner, slc, order, crew, jobs)
        return
    S = T.sem
    V, A = g.vector, g.scalar
    m, dests = slc[r], order[r]
    own_slot = T.ring[:, r * C:(r + 1) * C]
    mine = [[j for j in jobs if j[0] == w and j[1] == r] for w in range(len(WAVES))]
    mine = [sorted(js, key=lambda j: j[4]) for js in mine]
    off_chip = topo.mask(core, cores[dests[0]])

    k = 0
    for w, js in enumerate(mine):
        for j in js:
            t = slc[j[2]]
            (g.sync, A)[k % 2].dma_start(T.xs[t], T.x[:, C * t:C * t + C]).then_inc(S["ld%d" % w], 16)
            k += 1
            if k == 1:
                g.sync.dma_start(T.hhs[0:16, 0:2], T.hh[:]).then_inc(S.hl, 16)
    A.dma_start(own_slot, T.x[:, C * m:C * m + C]).then_inc(S.ldo, 16)

    g.iota(T.raw[:], [[16, 64]], 0, 0).then_inc(S.gi, 1)
    g.wait_ge(S.gi, 1)
    rid, pid = topo.addr(crew[r][-1], core)
    g.remote_dma(T.cols[:], T.raw[:], S.cnt, S.snt, pid, rid, sum(bits(topo.mask(core, crew[r][-1]))[:2 * NR]))
    sent = 2 * NR

    for w, js in enumerate(mine):
        g.wait_ge(S["ld%d" % w], 16 * len(js))
        tr = []
        for _, _, d, c, at, cnt, here in js:
            e = bits(topo.mask(core, c) & ~off_chip) if here else bits(topo.mask(core, c))
            tr.append(send(topo, core, c, sum(e[at:at + cnt]), S["arr%d" % w], T.xs[slc[d]], T.stage[w]))
            sent += cnt
        g.remote_dma_fused(tr, local_sem=S.snt)
    far = cores[partner[r]]
    rid, pid = topo.addr(far, core)
    g.wait_ge(S.ldo, 16)
    g.remote_dma(own_slot, own_slot, S.ringed, S.snt, pid, rid, sum(bits(topo.mask(core, far))[:NR]))
    sent += NR

    tabled = 2 * NR * len(TABLES)
    V.wait_ge(S.hl, 16)
    V.tensor_copy(T.hf[0:16, 0:1], T.hhs[0:16, 0:1]).then_inc(S.vl, 1)
    g.tensor.wait_ge(S.cst, tabled)
    g.tensor.wait_ge(S.vl, 1)
    g.tensor.matmul(T.hp[:, 0:1], T.sel[0:16, :], T.hf[0:16, 0:1], True, True).then_inc(S.mm, 1)
    V.wait_ge(S.cst, tabled)
    V.wait_ge(S.mm, 1)
    V.tensor_scalar(T.a1[:], T.t1[:], T.hp[:, 0:1], None, O.add).then_inc(S.vl, 1)
    V.wait_ge(S.vl, 2)
    V.tensor_scalar(T.b1[:], T.a1[:], 3, (N - 1) * C, O.arith_shift_right, O.bitwise_and).then_inc(S.vl, 1)
    V.wait_ge(S.vl, 3)
    V.tensor_tensor(T.d1[:], T.b1[:], T.tc[:], O.add).then_inc(S.vl, 1)
    V.wait_ge(S.vl, 4)
    V.tensor_copy(T.off1[:], T.d1[:]).then_inc(S.vl, 1)

    copy = ActivationFunctionType.Copy

    def by_v(out, win, off, a, b):
        return V.tensor_copy(out, win.indirect(off[:, a // 16:b // 16]))

    def by_a(out, win, off, a, b):
        return A.activation(out, win.indirect(off[:, a // 16:b // 16]), copy, bias=-0.0)

    filled = NR
    for _, _, d, c, _, _, _ in jobs:
        if r in (d, partner[d]):
            f, a = ways(topo, c, cores[d], cores[partner[d]])
            filled += len(a) if d == r else len(f)
    for q in (V, A):
        q.wait_ge(S.vl, 5)
        q.wait_ge(S.ldo, 16)
        q.wait_ge(S.ringed, filled)
    ring = T.ring[:, 0:N * C]
    lo = 0
    for j, (cnt, eng) in enumerate(CALLS3):
        hi = lo + C * cnt
        mid = lo + (hi - lo) // 64 * 32
        by_v(T.po[:, lo:mid], ring, T.off1, lo, mid).then_inc(S["c%d" % j], 1)
        by_a(T.po[:, mid:hi], ring, T.off1, mid, hi).then_inc(S["c%d" % j], 1)
        lo = hi
    by_v(T.v[:, m * C:(m + 1) * C], ring, T.off1, lo, W).then_inc(S.own, 1)

    e = 0
    for j, (cnt, eng) in enumerate(CALLS3):
        g.wait_ge(S["c%d" % j], 2)
        tr = []
        for _ in range(cnt):
            piece = T.po[:, e * C:(e + 1) * C]
            at = eng * len(tr)
            if e < RELAYED:
                c = crew[r][e]
                b = bits(topo.mask(core, c) & ~off_chip)[at:at + eng]
                tr.append(send(topo, core, c, sum(b), S.fwd, piece, T.fw[:]))
            else:
                c = cores[dests[e]]
                b = bits(topo.mask(core, c))[at:at + eng]
                tr.append(send(topo, core, c, sum(b), S.vin, piece, T.v[:, m * C:(m + 1) * C]))
            e += 1
        g.remote_dma_fused(tr, local_sem=S.snt)
        sent += eng * cnt

    V.wait_ge(S.ctt, 2 * NR)
    V.tensor_scalar(T.a2[:], T.t2[:], T.hp[:, 0:1], None, O.add).then_inc(S.vt, 1)
    V.wait_ge(S.vt, 1)
    V.tensor_scalar(T.b2[:], T.a2[:], W - 1, None, O.bitwise_and).then_inc(S.vt, 1)
    V.wait_ge(S.vt, 2)
    V.tensor_copy(T.off2[:], T.b2[:]).then_inc(S.vt, 1)

    got = NR * RELAYED + sum(cnt * eng for cnt, eng in CALLS3[1:])
    for q in (V, A):
        q.wait_ge(S.vt, 3)
        q.wait_ge(S.own, 1)
        q.wait_ge(S.vin, got)
    v = T.v[:, 0:W]
    parts = list(zip(CUTS, CUTS[1:]))
    for k, (a, b) in enumerate(parts):
        (by_v, by_a)[k % 2](T.yb[:, a:b], v, T.off2, a, b).then_inc(S["r%d" % k], 1)
    for k, (a, b) in enumerate(parts):
        q = A if k == len(parts) - 1 else g.sync
        q.wait_ge(S["r%d" % k], 1)
        q.dma_start(T.y[:, a:b], T.yb[:, a:b]).then_inc(S.st, 16)
    g.sync.wait_ge(S.st, 16 * len(parts))
    g.wait_ge(S.snt, sent)
